import numpy as np
import ml_dtypes


def mxq(x, axis, fmt="e4m3"):
    dtype, down = {"e4m3": (ml_dtypes.float8_e4m3fn, 7), "e5m2": (ml_dtypes.float8_e5m2, 14)}[fmt]
    v = np.moveaxis(np.asarray(x, np.float32).astype(ml_dtypes.bfloat16).astype(np.float64), axis, -1)
    blocks = v.reshape(v.shape[:-1] + (-1, 32))
    amax = np.abs(blocks).max(-1, keepdims=True)
    byte = np.maximum(np.where(amax > 0, np.frexp(amax)[1] - 1 + 127, 0) - down, 1)
    scale = np.exp2(byte - 127.0)
    codes = (blocks / scale).astype(np.float32).astype(dtype).astype(np.float64)
    return np.moveaxis((codes * scale).reshape(v.shape), -1, axis)


WIDE = False


def mx_kscale(k):
    if not WIDE:
        return np.ones(k)
    levels = np.array([10, -10, 5, -5, 0])
    if k % 512:
        return np.exp2(np.random.permutation(np.resize(levels, k // 32))).repeat(32)
    a = np.empty((k // 512, 16))
    for p in range(k // 512):
        a[p, :8] = np.random.permutation(np.resize(levels, 8))
        for g in range(8):
            far = levels[np.abs(levels - a[p, g]) >= 10]
            a[p, g + 8] = far[np.random.randint(len(far))]
    return np.exp2(a.ravel()).repeat(32)


def f64(x):
    return np.asarray(x).astype(np.float64)


def striped(idx):
    return np.tile(idx.reshape(-1, 16).T, (8, 1)).astype(np.uint16)


def unstriped(offs):
    return offs[:16].T.reshape(-1).astype(np.int64)


E2M1 = np.array([0.0, 0.5, 1.0, 1.5, 2.0, 3.0, 4.0, 6.0, -0.0, -0.5, -1.0, -1.5, -2.0, -3.0, -4.0, -6.0])


def pack_weight(w, fmt):
    k, n = w.shape
    w = f64(np.asarray(w, np.float32).astype(ml_dtypes.bfloat16)).reshape(k // 32, 32, n)
    amax = np.abs(w).max(1)
    if fmt == "e4m3":
        byte = np.frexp(amax)[1] - 1 + 127 - 7
    else:
        mant, ex = np.frexp(amax / 6.0)
        byte = np.where(mant > 0.5, ex, ex - 1) + 127
    byte = np.clip(np.where(amax > 0, byte, 1), 1, 254)
    scaled = (w * np.exp2(127.0 - byte)[:, None, :]).reshape(k, n).astype(np.float32)
    by_word = np.ascontiguousarray(scaled.reshape(k // 512, 128, 4, n).transpose(0, 1, 3, 2))
    if fmt == "e4m3":
        words = by_word.astype(ml_dtypes.float8_e4m3fn).view(np.uint8)
    else:
        c = by_word.astype(ml_dtypes.float4_e2m1fn).view(np.uint8) & 0xF
        words = (c[..., 0::2] | (c[..., 1::2] << 4)).reshape(k // 512, 128, 2 * n)
    return np.ascontiguousarray(words), np.ascontiguousarray(byte.astype(np.uint8).reshape(k // 512, 16, n))


def unpack_weight(words, scales, fmt):
    g, _, n = scales.shape
    words = np.ascontiguousarray(words).reshape(g, 128, n, -1)
    if fmt == "e4m3":
        vals = words.view(ml_dtypes.float8_e4m3fn).astype(np.float64)
    else:
        nib = np.empty((g, 128, n, 4), np.uint8)
        nib[..., 0::2] = words & 0xF
        nib[..., 1::2] = words >> 4
        vals = E2M1[nib]
    vals = vals * np.repeat(np.exp2(scales.astype(np.float64) - 127.0), 8, axis=1)[..., None]
    return vals.transpose(0, 1, 3, 2).reshape(g * 512, n)


def planes(y):
    n, m = y.shape
    v = y.astype(np.float32).astype(ml_dtypes.bfloat16).astype(np.float64).reshape(n // 32, 32, m)
    top = np.abs(v).max(1)
    byte = np.clip(np.where(top > 0, np.frexp(top)[1] - 1 + 127 - 7, 1), 1, 254)
    codes = (v * np.exp2(127.0 - byte)[:, None, :]).reshape(n, m).astype(np.float32).astype(ml_dtypes.float8_e4m3fn).view(np.uint8)
    words = codes.reshape(n // 512, 128, 4, m).transpose(0, 1, 3, 2)
    return np.ascontiguousarray(words), np.ascontiguousarray(byte.astype(np.uint8).reshape(n // 512, 16, m))


D, T, E, C, H, N = 2, 512, 8, 256, 512, 512


def by_expert(wq, xq):
    return np.concatenate([wq[e].T @ xq[:, e * C:(e + 1) * C] for e in range(E)], axis=1)


def setup_inputs():
    n = np.random.standard_normal
    s = np.tile(mx_kscale(H), D)
    u = mx_kscale(H)
    X = D * T
    first = np.random.permutation(np.repeat(np.arange(E), X // E))
    second = (first + 1 + np.random.permutation(np.repeat(np.arange(E - 1), -(-X // (E - 1)))[:X])) % E
    while np.bincount(second, minlength=E).max() != X // E:
        load = np.bincount(second, minlength=E); hi, lo = int(load.argmax()), int(load.argmin())
        t = np.flatnonzero((second == hi) & (first != lo))[0]; second[t] = lo
    slot_sub = np.empty(E * C, np.int64); pos = np.empty((2, X), np.int64); fill = np.zeros(E, np.int64)
    place = np.stack([np.random.permutation(C) for _ in range(E)])
    for r, deal in enumerate((first, second)):
        for t in np.random.permutation(X):
            e = deal[t]; j = e * C + place[e, fill[e]]; fill[e] += 1; slot_sub[j] = t; pos[r, t] = j
    g = np.random.uniform(0.2, 0.8, X)
    x = pack_weight(n((D * H, T)) * s[:, None], "e4m3")
    w = [pack_weight(m, "e2m1") for m in n((E, H, H)) / np.sqrt(H) / s[None, :H, None] * u]
    return {
        "x_words": x[0],
        "x_scales": x[1],
        "w_words": np.stack([m[0] for m in w]),
        "w_scales": np.stack([m[1] for m in w]),
        "wm": (n((D * H, N)) / np.sqrt(D * H) / np.tile(u, D)[:, None]).astype(np.float32),
        "gate": np.stack([np.tile(g, (128, 1)), np.tile(1.0 - g, (128, 1))]).astype(np.float32),
        "offs": striped(slot_sub),
        "pos1": striped(pos[0]),
        "pos2": striped(pos[1]),
    }


def reference(x_words, x_scales, w_words, w_scales, wm, gate, offs, pos1, pos2):
    w = np.stack([unpack_weight(w_words[e], w_scales[e], "e2m1") for e in range(E)])
    wmq = mxq(f64(wm), 0, "e4m3")
    idx = unstriped(offs)
    x = unpack_weight(x_words, x_scales, "e4m3")
    sub = x.reshape(D, H, T).transpose(1, 0, 2).reshape(H, D * T)
    y = by_expert(w, sub[:, idx])
    c = sum(f64(gate[r, :1]) * y[:, unstriped(p)] for r, p in enumerate((pos1, pos2)))
    cq = mxq(c, 0, "e4m3").reshape(H, D, T).transpose(1, 0, 2).reshape(D * H, T)
    out_0 = wmq.T @ cq
    return (out_0,) + planes(out_0)

@@ -1,0 +1,236 @@
+from contextlib import ExitStack
+
+import concourse.mybir as mybir
+
+F32 = mybir.dt.float32
+BF16 = mybir.dt.bfloat16
+I32 = mybir.dt.int32
+U32 = mybir.dt.uint32
+U16 = mybir.dt.uint16
+U8 = mybir.dt.uint8
+FP8X4 = mybir.dt.float8_e4m3fn_x4
+FP4X4 = mybir.dt.float4_e2m1fn_x4
+MULT = mybir.AluOpType.mult
+ADD = mybir.AluOpType.add
+COPY = mybir.ActivationFunctionType.Copy
+
+P = 128
+HEADS, TOKENS, EXPERTS, CAP, H, N = 2, 512, 8, 256, 512, 512
+SUBS = HEADS * TOKENS
+SLOTS = EXPERTS * CAP
+PACK = 4
+PAIRS = EXPERTS // 2
+PAIR_SLOTS = 2 * CAP
+UNIT = 128
+
+FLOPS = 2 * H * H * SLOTS + 2 * HEADS * H * N * TOKENS
+
+BLOCKS = (
+    (0, 0, 256, ((0, 0), (1, 0), (2, 0), (3, 0), (0, 1), (1, 1),)),
+    (1, 0, 256, ((0, 0), (1, 0),)),
+    (0, 256, 256, ((0, 0),)),
+    (1, 256, 128, ()),
+    (1, 384, 128, ((0, 0), (1, 0),)),
+)
+
+
+def tile_moe_mhm_none_kernel(
+    tc, x_words, x_scales, w_words, w_scales, wm, gate, offs, pos1, pos2, out_0, out_1, out_2
+):
+    nc = tc.nc
+    with ExitStack() as ctx:
+        keep = ctx.enter_context(tc.tile_pool(name="keep", bufs=1))
+        psum = ctx.enter_context(tc.psum_pool(name="psum", bufs=8))
+
+        def held(shape, dtype, name):
+            return keep.tile(shape, dtype, name=name, align_bytes=64)
+
+        offs_sb = held([P, SLOTS // 16], U16, "offs_sb")
+        pos_sb = [held([P, SUBS // 16], U16, "pos1_sb"), held([P, SUBS // 16], U16, "pos2_sb")]
+        xw = held([P, SUBS], I32, "xw")
+        xs = held([P, SUBS], U8, "xs")
+        ws_raw = keep.tile([P, EXPERTS * H], U8, name="ws_raw", tag="scales_then_wm", align_bytes=64)
+        nc.gpsimd.memset(xs[:].bitcast(I32), 0)
+        nc.vector.memset(ws_raw[:].bitcast(I32), 0)
+
+        nc.sync.dma_start(offs_sb[:], offs)
+        nc.sync.dma_start(pos_sb[0][:], pos1)
+        nc.sync.dma_start(pos_sb[1][:], pos2)
+        xs_rows = x_scales.rearrange("o (q i) t -> i q o t", i=4)
+        for i in range(4):
+            nc.sync.dma_start(
+                out=xs[i:P:32, :].bitcast(I32).rearrange("q (o t) -> q o t", o=HEADS),
+                in_=xs_rows[i].bitcast(I32),
+            )
+        w_rows = w_words.rearrange("e s p b -> p (e s) b").bitcast(I32)
+        ww_raw = []
+
+        def load_words(half, tag):
+            raw = keep.tile([P, 4, 256], I32, name="ww_raw%d" % half, tag=tag, align_bytes=64)
+            ww_raw.append(raw)
+            nc.sync.dma_start(out=raw[:], in_=w_rows[:, 4 * half : 4 * half + 4, :])
+
+        load_words(0, "words0_then_gate")
+        nc.sync.dma_start(
+            out=xw[:].rearrange("p (o t) -> p o t", o=HEADS),
+            in_=x_words.rearrange("o p t d -> p o (t d)").bitcast(I32),
+        )
+        ws_rows = w_scales.rearrange("e s (q i) l -> i q (e s) l", i=4)
+        for i in range(4):
+            nc.sync.dma_start(
+                out=ws_raw[i:P:32, :].bitcast(I32).rearrange("q (e l) -> q e l", e=EXPERTS),
+                in_=ws_rows[i].bitcast(I32),
+            )
+        load_words(1, "words1_then_wm")
+
+        ww = [held([P, 2 * 2 * H], U8, "ww%d" % c) for c in range(PAIRS)]
+        ws = [held([P, 2 * H], U8, "ws%d" % c) for c in range(PAIRS)]
+
+        def deal_words(c):
+            src = ww_raw[c // 2][:, 2 * (c % 2) : 2 * (c % 2) + 2, :].bitcast(U32)
+            nc.scalar.copy(
+                out=ww[c][:].bitcast(U32).rearrange("p (e b g r) -> p e b g r", e=2, b=4, r=2),
+                in_=src.rearrange("p e (g b r) -> p e b g r", b=4, r=2),
+            )
+
+        def deal_scales(c):
+            src = ws_raw[:, 2 * H * c : 2 * H * (c + 1)].bitcast(U32)
+            nc.scalar.copy(
+                out=ws[c][:].bitcast(U32).rearrange("p (e b g i) -> p e g b i", e=2, b=4, i=4),
+                in_=src.rearrange("p (e g i b) -> p e g b i", e=2, b=4, i=4),
+            )
+
+        xg = [held([P, PAIR_SLOTS], U32, "xg%d" % c) for c in range(PAIRS)]
+        sg = {}
+        y = [held([P, SLOTS], F32, "y%d" % b) for b in range(PACK)]
+        banks = {}
+
+        def gather_tokens(c):
+            cut = offs_sb[:, c * PAIR_SLOTS // 16 : (c + 1) * PAIR_SLOTS // 16]
+            sg[c] = keep.tile([P, PAIR_SLOTS], U8, name="sg", bufs=2, align_bytes=64)
+            nc.vector.tensor_copy(sg[c][:], xs[:].indirect(cut))
+            nc.vector.tensor_copy(xg[c][:], xw[:].bitcast(U32).indirect(cut))
+
+        def experts(c):
+            for b in range(PACK):
+                bank = psum.tile([P, PAIR_SLOTS], F32, name="bank")
+                banks[c, b] = bank
+                for e in range(2):
+                    col = e * H + b * P
+                    slots = slice(e * CAP, (e + 1) * CAP)
+                    nc.tensor.matmul_mx(
+                        out=bank[:, slots],
+                        lhsT=ww[c][:, 2 * col : 2 * (col + P)].bitcast(FP4X4),
+                        lhsT_scale=ws[c][:, col : col + P],
+                        rhs=xg[c][:, slots].bitcast(FP8X4),
+                        rhs_scale=sg[c][:, slots],
+                        start=True,
+                        stop=True,
+                    )
+
+        def empty(c, b):
+            nc.scalar.copy(out=y[b][:, c * PAIR_SLOTS : (c + 1) * PAIR_SLOTS], in_=banks[c, b][:])
+
+        deal_words(0)
+        deal_scales(0)
+        deal_words(1)
+        for c in range(1, PAIRS):
+            deal_scales(c)
+        deal_words(2)
+        deal_words(3)
+        gather_tokens(0)
+        gather_tokens(1)
+        for c in range(2):
+            experts(c)
+            gather_tokens(c + 2)
+            for b in range(PACK):
+                empty(c, b)
+        experts(2)
+        experts(3)
+        for b in range(PACK):
+            empty(2, b)
+            empty(3, b)
+
+        wm_codes = [held([P, N], U32, "wm_codes%d" % o) for o in range(HEADS)]
+        wm_scales = [held([P, N], U8, "wm_scales%d" % o) for o in range(HEADS)]
+        wm_rows = wm.rearrange("(o g j r) n -> o r g j n", o=HEADS, j=PACK, r=4)
+        gate_sb = keep.tile([P, 2, SUBS], F32, name="gate_sb", tag="words0_then_gate", align_bytes=64)
+        nc.sync.dma_start(out=gate_sb[:], in_=gate.rearrange("r p z -> p r z"))
+        wm_raw = []
+        for o, tag in enumerate(("scales_then_wm", "words1_then_wm")):
+            raw = keep.tile([P, PACK * N], F32, name="wm_raw%d" % o, tag=tag, align_bytes=64)
+            wm_raw.append(raw[:])
+            for r in range(4):
+                nc.sync.dma_start(out=raw[r:P:4, :].rearrange("g (j n) -> g j n", j=PACK), in_=wm_rows[o, r])
+        wm_bf = [held([P, N * PACK], BF16, "wm_bf%d" % o) for o in range(HEADS)]
+        for o in range(HEADS):
+            nc.vector.tensor_copy(
+                out=wm_bf[o][:].rearrange("p (s m j) -> p m j s", s=PACK, j=PACK),
+                in_=wm_raw[o].rearrange("p (j m s) -> p m j s", j=PACK, s=PACK),
+            )
+        for o in range(HEADS):
+            nc.vector.quantize_mx(out=wm_codes[o][:].bitcast(FP8X4), scales=wm_scales[o][:], in_=wm_bf[o][:])
+
+        out32 = held([P, PACK, TOKENS], F32, "out32")
+        out_words = held([P, TOKENS], U32, "out_words")
+        out_scales = held([P, TOKENS], U8, "out_scales")
+        out_rows = out_0.rearrange("(p s) t -> p s t", s=PACK)
+        word_rows = out_1[0].rearrange("p t d -> p (t d)").bitcast(I32)
+        acc = [psum.tile([P, PACK * UNIT], F32, name="bank") for u in range(TOKENS // UNIT)]
+
+        for k, (o, first, width, fused) in enumerate(BLOCKS):
+            z0 = o * TOKENS + first
+            zs = slice(z0, z0 + width)
+            picked = keep.tile([P, PACK, 2, width], F32, name="picked", bufs=2, align_bytes=64)
+            gated = held([P, PACK, 2, width], F32, "gated%d" % k)
+            for b in range(PACK):
+                for r in range(2):
+                    window = y[b][:].indirect(pos_sb[r][:, z0 // 16 : (z0 + width) // 16])
+                    if (b, r) in fused:
+                        nc.vector.tensor_tensor(gated[:, b, r, :], window, gate_sb[:, r, zs], MULT)
+                    else:
+                        nc.scalar.activation(picked[:, b, r, :], window, COPY)
+                plain = [r for r in range(2) if (b, r) not in fused]
+                if plain:
+                    rs = slice(plain[0], plain[-1] + 1)
+                    nc.vector.tensor_tensor(gated[:, b, rs, :], picked[:, b, rs, :], gate_sb[:, rs, zs], MULT)
+            c_bf = held([P, width * PACK], BF16, "c_bf%d" % k)
+            nc.vector.tensor_tensor(
+                c_bf[:].rearrange("p (c i b) -> p c b i", i=2, b=PACK),
+                gated[:, :, 0, :].rearrange("p b (c i) -> p c b i", i=2),
+                gated[:, :, 1, :].rearrange("p b (c i) -> p c b i", i=2),
+                ADD,
+            )
+            c_codes = held([P, width], U32, "c_codes%d" % k)
+            c_scales = held([P, width], U8, "c_scales%d" % k)
+            nc.vector.quantize_mx(out=c_codes[:].bitcast(FP8X4), scales=c_scales[:], in_=c_bf[:])
+            for u in range(first // UNIT, (first + width) // UNIT):
+                cols = slice(u * UNIT - first, (u + 1) * UNIT - first)
+                for s in range(PACK):
+                    nc.tensor.matmul_mx(
+                        out=acc[u][:, s * UNIT : (s + 1) * UNIT],
+                        lhsT=wm_codes[o][:, s * P : (s + 1) * P].bitcast(FP8X4),
+                        lhsT_scale=wm_scales[o][:, s * P : (s + 1) * P],
+                        rhs=c_codes[:, cols].bitcast(FP8X4),
+                        rhs_scale=c_scales[:, cols],
+                        start=(o == 0 and s == 0),
+                        stop=(o == HEADS - 1 and s == PACK - 1),
+                    )
+                if o == HEADS - 1:
+                    tok = slice(u * UNIT, (u + 1) * UNIT)
+                    out_bf = held([P, UNIT * PACK], BF16, "out_bf%d" % u)
+                    nc.scalar.copy(
+                        out=out_bf[:].rearrange("p (t s) -> p t s", s=PACK),
+                        in_=acc[u][:].rearrange("p (s t) -> p t s", s=PACK),
+                    )
+                    nc.scalar.copy(out=out32[:, :, tok], in_=acc[u][:].rearrange("p (s t) -> p s t", s=PACK))
+                    nc.vector.quantize_mx(
+                        out=out_words[:, tok].bitcast(FP8X4), scales=out_scales[:, tok], in_=out_bf[:]
+                    )
+            if o == HEADS - 1:
+                tok = slice(first, first + width)
+                nc.sync.dma_start(out=out_rows[:, :, tok], in_=out32[:, :, tok])
+                nc.sync.dma_start(out=word_rows[:, tok], in_=out_words[:, tok].bitcast(I32))
+        scale_rows = out_2[0].rearrange("(q i) t -> i q t", i=4)
+        for i in range(4):
+            nc.sync.dma_start(out=scale_rows[i].bitcast(I32), in_=out_scales[i:P:32, :].bitcast(I32))

@@ -28,10 +28,12 @@ FLOPS = 2 * H * H * SLOTS + 2 * HEADS * H * N * TOKENS
 BLOCKS = (
     (0, 0, 256, ((0, 0), (1, 0), (2, 0), (3, 0), (0, 1), (1, 1),)),
     (1, 0, 256, ((0, 0), (1, 0),)),
-    (0, 256, 256, ((0, 0),)),
+    (0, 256, 256, ((0, 0), (1, 0),)),
     (1, 256, 128, ()),
-    (1, 384, 128, ((0, 0), (1, 0),)),
+    (1, 384, 128, ()),
 )
+VECTOR_EMPTIES = ((3, 1), (3, 3))
+OUT_PARTS = ((0, 256), (256, 128), (384, 128))
 
 
 def tile_moe_mhm_none_kernel(
@@ -55,7 +57,6 @@ def tile_moe_mhm_none_kernel(
 
         nc.sync.dma_start(offs_sb[:], offs)
         nc.sync.dma_start(pos_sb[0][:], pos1)
-        nc.sync.dma_start(pos_sb[1][:], pos2)
         xs_rows = x_scales.rearrange("o (q i) t -> i q o t", i=4)
         for i in range(4):
             nc.sync.dma_start(
@@ -70,18 +71,19 @@ def tile_moe_mhm_none_kernel(
             ww_raw.append(raw)
             nc.sync.dma_start(out=raw[:], in_=w_rows[:, 4 * half : 4 * half + 4, :])
 
-        load_words(0, "words0_then_gate")
         nc.sync.dma_start(
             out=xw[:].rearrange("p (o t) -> p o t", o=HEADS),
             in_=x_words.rearrange("o p t d -> p o (t d)").bitcast(I32),
         )
+        load_words(0, "words0_then_wm")
         ws_rows = w_scales.rearrange("e s (q i) l -> i q (e s) l", i=4)
         for i in range(4):
             nc.sync.dma_start(
                 out=ws_raw[i:P:32, :].bitcast(I32).rearrange("q (e l) -> q e l", e=EXPERTS),
                 in_=ws_rows[i].bitcast(I32),
             )
-        load_words(1, "words1_then_wm")
+        load_words(1, "words1_then_gate")
+        nc.sync.dma_start(pos_sb[1][:], pos2)
 
         ww = [held([P, 2 * 2 * H], U8, "ww%d" % c) for c in range(PAIRS)]
         ws = [held([P, 2 * H], U8, "ws%d" % c) for c in range(PAIRS)]
@@ -95,7 +97,7 @@ def tile_moe_mhm_none_kernel(
 
         def deal_scales(c):
             src = ws_raw[:, 2 * H * c : 2 * H * (c + 1)].bitcast(U32)
-            nc.scalar.copy(
+            nc.gpsimd.tensor_copy(
                 out=ws[c][:].bitcast(U32).rearrange("p (e b g i) -> p e g b i", e=2, b=4, i=4),
                 in_=src.rearrange("p (e g i b) -> p e g b i", e=2, b=4, i=4),
             )
@@ -129,7 +131,8 @@ def tile_moe_mhm_none_kernel(
                     )
 
         def empty(c, b):
-            nc.scalar.copy(out=y[b][:, c * PAIR_SLOTS : (c + 1) * PAIR_SLOTS], in_=banks[c, b][:])
+            move = nc.vector.tensor_copy if (c, b) in VECTOR_EMPTIES else nc.scalar.copy
+            move(out=y[b][:, c * PAIR_SLOTS : (c + 1) * PAIR_SLOTS], in_=banks[c, b][:])
 
         deal_words(0)
         deal_scales(0)
@@ -154,19 +157,23 @@ def tile_moe_mhm_none_kernel(
         wm_codes = [held([P, N], U32, "wm_codes%d" % o) for o in range(HEADS)]
         wm_scales = [held([P, N], U8, "wm_scales%d" % o) for o in range(HEADS)]
         wm_rows = wm.rearrange("(o g j r) n -> o r g j n", o=HEADS, j=PACK, r=4)
-        gate_sb = keep.tile([P, 2, SUBS], F32, name="gate_sb", tag="words0_then_gate", align_bytes=64)
-        nc.sync.dma_start(out=gate_sb[:], in_=gate.rearrange("r p z -> p r z"))
         wm_raw = []
-        for o, tag in enumerate(("scales_then_wm", "words1_then_wm")):
+        for o, tag in enumerate(("words0_then_wm", "scales_then_wm")):
             raw = keep.tile([P, PACK * N], F32, name="wm_raw%d" % o, tag=tag, align_bytes=64)
             wm_raw.append(raw[:])
             for r in range(4):
                 nc.sync.dma_start(out=raw[r:P:4, :].rearrange("g (j n) -> g j n", j=PACK), in_=wm_rows[o, r])
+        gate_sb = keep.tile([P, 2, SUBS], F32, name="gate_sb", tag="words1_then_gate", align_bytes=64)
+        nc.sync.dma_start(out=gate_sb[:], in_=gate.rearrange("r p z -> p r z"))
         wm_bf = [held([P, N * PACK], BF16, "wm_bf%d" % o) for o in range(HEADS)]
         for o in range(HEADS):
-            nc.vector.tensor_copy(
-                out=wm_bf[o][:].rearrange("p (s m j) -> p m j s", s=PACK, j=PACK),
-                in_=wm_raw[o].rearrange("p (j m s) -> p m j s", j=PACK, s=PACK),
+            nc.gpsimd.tensor_scalar(
+                wm_bf[o][:].rearrange("p (s m j) -> p m s j", s=PACK, j=PACK),
+                wm_raw[o].rearrange("p (j m s) -> p m s j", j=PACK, s=PACK),
+                1.0,
+                0.0,
+                MULT,
+                ADD,
             )
         for o in range(HEADS):
             nc.vector.quantize_mx(out=wm_codes[o][:].bitcast(FP8X4), scales=wm_scales[o][:], in_=wm_bf[o][:])
@@ -181,19 +188,25 @@ def tile_moe_mhm_none_kernel(
         for k, (o, first, width, fused) in enumerate(BLOCKS):
             z0 = o * TOKENS + first
             zs = slice(z0, z0 + width)
-            picked = keep.tile([P, PACK, 2, width], F32, name="picked", bufs=2, align_bytes=64)
+            picked = held([P, PACK, 2, width], F32, "picked%d" % k)
             gated = held([P, PACK, 2, width], F32, "gated%d" % k)
-            for b in range(PACK):
-                for r in range(2):
-                    window = y[b][:].indirect(pos_sb[r][:, z0 // 16 : (z0 + width) // 16])
-                    if (b, r) in fused:
-                        nc.vector.tensor_tensor(gated[:, b, r, :], window, gate_sb[:, r, zs], MULT)
-                    else:
-                        nc.scalar.activation(picked[:, b, r, :], window, COPY)
-                plain = [r for r in range(2) if (b, r) not in fused]
+            for b0 in range(0, PACK, 2):
+                for b in (b0, b0 + 1):
+                    for r in range(2):
+                        window = y[b][:].indirect(pos_sb[r][:, z0 // 16 : (z0 + width) // 16])
+                        if (b, r) in fused:
+                            nc.vector.tensor_tensor(gated[:, b, r, :], window, gate_sb[:, r, zs], MULT)
+                        else:
+                            nc.scalar.activation(picked[:, b, r, :], window, COPY)
+                plain = [r for r in range(2) if (b0, r) not in fused]
                 if plain:
                     rs = slice(plain[0], plain[-1] + 1)
-                    nc.vector.tensor_tensor(gated[:, b, rs, :], picked[:, b, rs, :], gate_sb[:, rs, zs], MULT)
+                    nc.vector.tensor_tensor(
+                        gated[:, b0 : b0 + 2, rs, :],
+                        picked[:, b0 : b0 + 2, rs, :],
+                        gate_sb[:, rs, zs].unsqueeze(1).to_broadcast([P, 2, len(plain), width]),
+                        MULT,
+                    )
             c_bf = held([P, width * PACK], BF16, "c_bf%d" % k)
             nc.vector.tensor_tensor(
                 c_bf[:].rearrange("p (c i b) -> p c b i", i=2, b=PACK),
@@ -216,21 +229,24 @@ def tile_moe_mhm_none_kernel(
                         start=(o == 0 and s == 0),
                         stop=(o == HEADS - 1 and s == PACK - 1),
                     )
-                if o == HEADS - 1:
-                    tok = slice(u * UNIT, (u + 1) * UNIT)
-                    out_bf = held([P, UNIT * PACK], BF16, "out_bf%d" % u)
-                    nc.scalar.copy(
-                        out=out_bf[:].rearrange("p (t s) -> p t s", s=PACK),
-                        in_=acc[u][:].rearrange("p (s t) -> p t s", s=PACK),
-                    )
-                    nc.scalar.copy(out=out32[:, :, tok], in_=acc[u][:].rearrange("p (s t) -> p s t", s=PACK))
-                    nc.vector.quantize_mx(
-                        out=out_words[:, tok].bitcast(FP8X4), scales=out_scales[:, tok], in_=out_bf[:]
-                    )
-            if o == HEADS - 1:
-                tok = slice(first, first + width)
-                nc.sync.dma_start(out=out_rows[:, :, tok], in_=out32[:, :, tok])
-                nc.sync.dma_start(out=word_rows[:, tok], in_=out_words[:, tok].bitcast(I32))
+
+        for first, width in OUT_PARTS:
+            tok = slice(first, first + width)
+            units = range(first // UNIT, (first + width) // UNIT)
+            out_bf = held([P, width * PACK], BF16, "out_bf%d" % first)
+            for u in units:
+                at = (u * UNIT - first) * PACK
+                nc.scalar.copy(
+                    out=out_bf[:, at : at + UNIT * PACK].rearrange("p (t s) -> p t s", s=PACK),
+                    in_=acc[u][:].rearrange("p (s t) -> p t s", s=PACK),
+                )
+            nc.vector.quantize_mx(out=out_words[:, tok].bitcast(FP8X4), scales=out_scales[:, tok], in_=out_bf[:])
+            nc.sync.dma_start(out=word_rows[:, tok], in_=out_words[:, tok].bitcast(I32))
+            for u in units:
+                nc.scalar.copy(
+                    out=out32[:, :, u * UNIT : (u + 1) * UNIT], in_=acc[u][:].rearrange("p (s t) -> p s t", s=PACK)
+                )
+            nc.sync.dma_start(out=out_rows[:, :, tok], in_=out32[:, :, tok])
         scale_rows = out_2[0].rearrange("(q i) t -> i q t", i=4)
         for i in range(4):
             nc.sync.dma_start(out=scale_rows[i].bitcast(I32), in_=out_scales[i:P:32, :].bitcast(I32))

@@ -32,7 +32,7 @@ BLOCKS = (
     (1, 256, 128, ()),
     (1, 384, 128, ()),
 )
-VECTOR_EMPTIES = ((3, 1), (3, 3))
+VECTOR_EMPTIES = ((3, 0), (3, 1))
 OUT_PARTS = ((0, 256), (256, 128), (384, 128))
 
 
@@ -51,9 +51,10 @@ def tile_moe_mhm_none_kernel(
         pos_sb = [held([P, SUBS // 16], U16, "pos1_sb"), held([P, SUBS // 16], U16, "pos2_sb")]
         xw = held([P, SUBS], I32, "xw")
         xs = held([P, SUBS], U8, "xs")
-        ws_raw = keep.tile([P, EXPERTS * H], U8, name="ws_raw", tag="scales_then_wm", align_bytes=64)
+        ws_raw = keep.tile([P, EXPERTS * H], U8, name="ws_raw", align_bytes=64)
         nc.gpsimd.memset(xs[:].bitcast(I32), 0)
-        nc.vector.memset(ws_raw[:].bitcast(I32), 0)
+        nc.vector.memset(ws_raw[:, 0 : 6 * H].bitcast(I32), 0)
+        nc.gpsimd.memset(ws_raw[:, 6 * H :].bitcast(I32), 0)
 
         nc.sync.dma_start(offs_sb[:], offs)
         nc.sync.dma_start(pos_sb[0][:], pos1)
@@ -66,8 +67,8 @@ def tile_moe_mhm_none_kernel(
         w_rows = w_words.rearrange("e s p b -> p (e s) b").bitcast(I32)
         ww_raw = []
 
-        def load_words(half, tag):
-            raw = keep.tile([P, 4, 256], I32, name="ww_raw%d" % half, tag=tag, align_bytes=64)
+        def load_words(half):
+            raw = keep.tile([P, 4, 256], I32, name="ww_raw%d" % half, align_bytes=64)
             ww_raw.append(raw)
             nc.sync.dma_start(out=raw[:], in_=w_rows[:, 4 * half : 4 * half + 4, :])
 
@@ -75,16 +76,25 @@ def tile_moe_mhm_none_kernel(
             out=xw[:].rearrange("p (o t) -> p o t", o=HEADS),
             in_=x_words.rearrange("o p t d -> p o (t d)").bitcast(I32),
         )
-        load_words(0, "words0_then_wm")
+        load_words(0)
         ws_rows = w_scales.rearrange("e s (q i) l -> i q (e s) l", i=4)
         for i in range(4):
             nc.sync.dma_start(
                 out=ws_raw[i:P:32, :].bitcast(I32).rearrange("q (e l) -> q e l", e=EXPERTS),
                 in_=ws_rows[i].bitcast(I32),
             )
-        load_words(1, "words1_then_gate")
+        load_words(1)
         nc.sync.dma_start(pos_sb[1][:], pos2)
 
+        wm_rows = wm.rearrange("(o g j r) n -> o r g j n", o=HEADS, j=PACK, r=4)
+        wm_raw = []
+        for o in range(HEADS):
+            raw = keep.tile([P, PACK * N], F32, name="wm_raw%d" % o, align_bytes=64)
+            wm_raw.append(raw[:])
+            for r in range(4):
+                nc.sync.dma_start(out=raw[r:P:4, :].rearrange("g (j n) -> g j n", j=PACK), in_=wm_rows[o, r])
+        gate_sb = keep.tile([P, 2, SUBS], F32, name="gate_sb", align_bytes=64)
+        nc.sync.dma_start(out=gate_sb[:], in_=gate.rearrange("r p z -> p r z"))
         ww = [held([P, 2 * 2 * H], U8, "ww%d" % c) for c in range(PAIRS)]
         ws = [held([P, 2 * H], U8, "ws%d" % c) for c in range(PAIRS)]
 
@@ -156,15 +166,6 @@ def tile_moe_mhm_none_kernel(
 
         wm_codes = [held([P, N], U32, "wm_codes%d" % o) for o in range(HEADS)]
         wm_scales = [held([P, N], U8, "wm_scales%d" % o) for o in range(HEADS)]
-        wm_rows = wm.rearrange("(o g j r) n -> o r g j n", o=HEADS, j=PACK, r=4)
-        wm_raw = []
-        for o, tag in enumerate(("words0_then_wm", "scales_then_wm")):
-            raw = keep.tile([P, PACK * N], F32, name="wm_raw%d" % o, tag=tag, align_bytes=64)
-            wm_raw.append(raw[:])
-            for r in range(4):
-                nc.sync.dma_start(out=raw[r:P:4, :].rearrange("g (j n) -> g j n", j=PACK), in_=wm_rows[o, r])
-        gate_sb = keep.tile([P, 2, SUBS], F32, name="gate_sb", tag="words1_then_gate", align_bytes=64)
-        nc.sync.dma_start(out=gate_sb[:], in_=gate.rearrange("r p z -> p r z"))
         wm_bf = [held([P, N * PACK], BF16, "wm_bf%d" % o) for o in range(HEADS)]
         for o in range(HEADS):
             nc.gpsimd.tensor_scalar(
@@ -246,7 +247,9 @@ def tile_moe_mhm_none_kernel(
                 nc.scalar.copy(
                     out=out32[:, :, u * UNIT : (u + 1) * UNIT], in_=acc[u][:].rearrange("p (s t) -> p s t", s=PACK)
                 )
-            nc.sync.dma_start(out=out_rows[:, :, tok], in_=out32[:, :, tok])
+            queue = nc.scalar if first + width == TOKENS else nc.sync
+            queue.dma_start(out=out_rows[:, :, tok], in_=out32[:, :, tok])
         scale_rows = out_2[0].rearrange("(q i) t -> i q t", i=4)
         for i in range(4):
-            nc.sync.dma_start(out=scale_rows[i].bitcast(I32), in_=out_scales[i:P:32, :].bitcast(I32))
+            queue = nc.sync if i < 2 else nc.scalar
+            queue.dma_start(out=scale_rows[i].bitcast(I32), in_=out_scales[i:P:32, :].bitcast(I32))

from contextlib import ExitStack

import concourse.mybir as mybir

F32 = mybir.dt.float32
BF16 = mybir.dt.bfloat16
I32 = mybir.dt.int32
U32 = mybir.dt.uint32
U16 = mybir.dt.uint16
U8 = mybir.dt.uint8
FP8X4 = mybir.dt.float8_e4m3fn_x4
FP4X4 = mybir.dt.float4_e2m1fn_x4
MULT = mybir.AluOpType.mult
ADD = mybir.AluOpType.add
COPY = mybir.ActivationFunctionType.Copy

P = 128
HEADS, TOKENS, EXPERTS, CAP, H, N = 2, 512, 8, 256, 512, 512
SUBS = HEADS * TOKENS
SLOTS = EXPERTS * CAP
PACK = 4
PAIRS = EXPERTS // 2
PAIR_SLOTS = 2 * CAP
UNIT = 128

FLOPS = 2 * H * H * SLOTS + 2 * HEADS * H * N * TOKENS

BLOCKS = (
    (0, 0, 256, ((0, 0), (1, 0), (2, 0), (3, 0), (0, 1), (1, 1),)),
    (1, 0, 256, ((0, 0), (1, 0),)),
    (0, 256, 256, ((0, 0), (1, 0),)),
    (1, 256, 128, ()),
    (1, 384, 128, ()),
)
VECTOR_EMPTIES = ((3, 0), (3, 1))
OUT_PARTS = ((0, 256), (256, 128), (384, 128))


def tile_moe_mhm_none_kernel(
    tc, x_words, x_scales, w_words, w_scales, wm, gate, offs, pos1, pos2, out_0, out_1, out_2
):
    nc = tc.nc
    with ExitStack() as ctx:
        keep = ctx.enter_context(tc.tile_pool(name="keep", bufs=1))
        psum = ctx.enter_context(tc.psum_pool(name="psum", bufs=8))

        def held(shape, dtype, name):
            return keep.tile(shape, dtype, name=name, align_bytes=64)

        offs_sb = held([P, SLOTS // 16], U16, "offs_sb")
        pos_sb = [held([P, SUBS // 16], U16, "pos1_sb"), held([P, SUBS // 16], U16, "pos2_sb")]
        xw = held([P, SUBS], I32, "xw")
        xs = held([P, SUBS], U8, "xs")
        ws_raw = keep.tile([P, EXPERTS * H], U8, name="ws_raw", align_bytes=64)
        nc.gpsimd.memset(xs[:].bitcast(I32), 0)
        nc.vector.memset(ws_raw[:, 0 : 6 * H].bitcast(I32), 0)
        nc.gpsimd.memset(ws_raw[:, 6 * H :].bitcast(I32), 0)

        nc.sync.dma_start(offs_sb[:], offs)
        nc.sync.dma_start(pos_sb[0][:], pos1)
        xs_rows = x_scales.rearrange("o (q i) t -> i q o t", i=4)
        for i in range(4):
            nc.sync.dma_start(
                out=xs[i:P:32, :].bitcast(I32).rearrange("q (o t) -> q o t", o=HEADS),
                in_=xs_rows[i].bitcast(I32),
            )
        w_rows = w_words.rearrange("e s p b -> p (e s) b").bitcast(I32)
        ww_raw = []

        def load_words(half):
            raw = keep.tile([P, 4, 256], I32, name="ww_raw%d" % half, align_bytes=64)
            ww_raw.append(raw)
            nc.sync.dma_start(out=raw[:], in_=w_rows[:, 4 * half : 4 * half + 4, :])

        nc.sync.dma_start(
            out=xw[:].rearrange("p (o t) -> p o t", o=HEADS),
            in_=x_words.rearrange("o p t d -> p o (t d)").bitcast(I32),
        )
        load_words(0)
        ws_rows = w_scales.rearrange("e s (q i) l -> i q (e s) l", i=4)
        for i in range(4):
            nc.sync.dma_start(
                out=ws_raw[i:P:32, :].bitcast(I32).rearrange("q (e l) -> q e l", e=EXPERTS),
                in_=ws_rows[i].bitcast(I32),
            )
        load_words(1)
        nc.sync.dma_start(pos_sb[1][:], pos2)

        wm_rows = wm.rearrange("(o g j r) n -> o r g j n", o=HEADS, j=PACK, r=4)
        wm_raw = []
        for o in range(HEADS):
            raw = keep.tile([P, PACK * N], F32, name="wm_raw%d" % o, align_bytes=64)
            wm_raw.append(raw[:])
            for r in range(4):
                nc.sync.dma_start(out=raw[r:P:4, :].rearrange("g (j n) -> g j n", j=PACK), in_=wm_rows[o, r])
        gate_sb = keep.tile([P, 2, SUBS], F32, name="gate_sb", align_bytes=64)
        nc.sync.dma_start(out=gate_sb[:], in_=gate.rearrange("r p z -> p r z"))
        ww = [held([P, 2 * 2 * H], U8, "ww%d" % c) for c in range(PAIRS)]
        ws = [held([P, 2 * H], U8, "ws%d" % c) for c in range(PAIRS)]

        def deal_words(c):
            src = ww_raw[c // 2][:, 2 * (c % 2) : 2 * (c % 2) + 2, :].bitcast(U32)
            nc.scalar.copy(
                out=ww[c][:].bitcast(U32).rearrange("p (e b g r) -> p e b g r", e=2, b=4, r=2),
                in_=src.rearrange("p e (g b r) -> p e b g r", b=4, r=2),
            )

        def deal_scales(c):
            src = ws_raw[:, 2 * H * c : 2 * H * (c + 1)].bitcast(U32)
            nc.gpsimd.tensor_copy(
                out=ws[c][:].bitcast(U32).rearrange("p (e b g i) -> p e g b i", e=2, b=4, i=4),
                in_=src.rearrange("p (e g i b) -> p e g b i", e=2, b=4, i=4),
            )

        xg = [held([P, PAIR_SLOTS], U32, "xg%d" % c) for c in range(PAIRS)]
        sg = {}
        y = [held([P, SLOTS], F32, "y%d" % b) for b in range(PACK)]
        banks = {}

        def gather_tokens(c):
            cut = offs_sb[:, c * PAIR_SLOTS // 16 : (c + 1) * PAIR_SLOTS // 16]
            sg[c] = keep.tile([P, PAIR_SLOTS], U8, name="sg", bufs=2, align_bytes=64)
            nc.vector.tensor_copy(sg[c][:], xs[:].indirect(cut))
            nc.vector.tensor_copy(xg[c][:], xw[:].bitcast(U32).indirect(cut))

        def experts(c):
            for b in range(PACK):
                bank = psum.tile([P, PAIR_SLOTS], F32, name="bank")
                banks[c, b] = bank
                for e in range(2):
                    col = e * H + b * P
                    slots = slice(e * CAP, (e + 1) * CAP)
                    nc.tensor.matmul_mx(
                        out=bank[:, slots],
                        lhsT=ww[c][:, 2 * col : 2 * (col + P)].bitcast(FP4X4),
                        lhsT_scale=ws[c][:, col : col + P],
                        rhs=xg[c][:, slots].bitcast(FP8X4),
                        rhs_scale=sg[c][:, slots],
                        start=True,
                        stop=True,
                    )

        def empty(c, b):
            move = nc.vector.tensor_copy if (c, b) in VECTOR_EMPTIES else nc.scalar.copy
            move(out=y[b][:, c * PAIR_SLOTS : (c + 1) * PAIR_SLOTS], in_=banks[c, b][:])

        deal_words(0)
        deal_scales(0)
        deal_words(1)
        for c in range(1, PAIRS):
            deal_scales(c)
        deal_words(2)
        deal_words(3)
        gather_tokens(0)
        gather_tokens(1)
        for c in range(2):
            experts(c)
            gather_tokens(c + 2)
            for b in range(PACK):
                empty(c, b)
        experts(2)
        experts(3)
        for b in range(PACK):
            empty(2, b)
            empty(3, b)

        wm_codes = [held([P, N], U32, "wm_codes%d" % o) for o in range(HEADS)]
        wm_scales = [held([P, N], U8, "wm_scales%d" % o) for o in range(HEADS)]
        wm_bf = [held([P, N * PACK], BF16, "wm_bf%d" % o) for o in range(HEADS)]
        for o in range(HEADS):
            nc.gpsimd.tensor_scalar(
                wm_bf[o][:].rearrange("p (s m j) -> p m s j", s=PACK, j=PACK),
                wm_raw[o].rearrange("p (j m s) -> p m s j", j=PACK, s=PACK),
                1.0,
                0.0,
                MULT,
                ADD,
            )
        for o in range(HEADS):
            nc.vector.quantize_mx(out=wm_codes[o][:].bitcast(FP8X4), scales=wm_scales[o][:], in_=wm_bf[o][:])

        out32 = held([P, PACK, TOKENS], F32, "out32")
        out_words = held([P, TOKENS], U32, "out_words")
        out_scales = held([P, TOKENS], U8, "out_scales")
        out_rows = out_0.rearrange("(p s) t -> p s t", s=PACK)
        word_rows = out_1[0].rearrange("p t d -> p (t d)").bitcast(I32)
        acc = [psum.tile([P, PACK * UNIT], F32, name="bank") for u in range(TOKENS // UNIT)]

        for k, (o, first, width, fused) in enumerate(BLOCKS):
            z0 = o * TOKENS + first
            zs = slice(z0, z0 + width)
            picked = held([P, PACK, 2, width], F32, "picked%d" % k)
            gated = held([P, PACK, 2, width], F32, "gated%d" % k)
            for b0 in range(0, PACK, 2):
                for b in (b0, b0 + 1):
                    for r in range(2):
                        window = y[b][:].indirect(pos_sb[r][:, z0 // 16 : (z0 + width) // 16])
                        if (b, r) in fused:
                            nc.vector.tensor_tensor(gated[:, b, r, :], window, gate_sb[:, r, zs], MULT)
                        else:
                            nc.scalar.activation(picked[:, b, r, :], window, COPY)
                plain = [r for r in range(2) if (b0, r) not in fused]
                if plain:
                    rs = slice(plain[0], plain[-1] + 1)
                    nc.vector.tensor_tensor(
                        gated[:, b0 : b0 + 2, rs, :],
                        picked[:, b0 : b0 + 2, rs, :],
                        gate_sb[:, rs, zs].unsqueeze(1).to_broadcast([P, 2, len(plain), width]),
                        MULT,
                    )
            c_bf = held([P, width * PACK], BF16, "c_bf%d" % k)
            nc.vector.tensor_tensor(
                c_bf[:].rearrange("p (c i b) -> p c b i", i=2, b=PACK),
                gated[:, :, 0, :].rearrange("p b (c i) -> p c b i", i=2),
                gated[:, :, 1, :].rearrange("p b (c i) -> p c b i", i=2),
                ADD,
            )
            c_codes = held([P, width], U32, "c_codes%d" % k)
            c_scales = held([P, width], U8, "c_scales%d" % k)
            nc.vector.quantize_mx(out=c_codes[:].bitcast(FP8X4), scales=c_scales[:], in_=c_bf[:])
            for u in range(first // UNIT, (first + width) // UNIT):
                cols = slice(u * UNIT - first, (u + 1) * UNIT - first)
                for s in range(PACK):
                    nc.tensor.matmul_mx(
                        out=acc[u][:, s * UNIT : (s + 1) * UNIT],
                        lhsT=wm_codes[o][:, s * P : (s + 1) * P].bitcast(FP8X4),
                        lhsT_scale=wm_scales[o][:, s * P : (s + 1) * P],
                        rhs=c_codes[:, cols].bitcast(FP8X4),
                        rhs_scale=c_scales[:, cols],
                        start=(o == 0 and s == 0),
                        stop=(o == HEADS - 1 and s == PACK - 1),
                    )

        for first, width in OUT_PARTS:
            tok = slice(first, first + width)
            units = range(first // UNIT, (first + width) // UNIT)
            out_bf = held([P, width * PACK], BF16, "out_bf%d" % first)
            for u in units:
                at = (u * UNIT - first) * PACK
                nc.scalar.copy(
                    out=out_bf[:, at : at + UNIT * PACK].rearrange("p (t s) -> p t s", s=PACK),
                    in_=acc[u][:].rearrange("p (s t) -> p t s", s=PACK),
                )
            nc.vector.quantize_mx(out=out_words[:, tok].bitcast(FP8X4), scales=out_scales[:, tok], in_=out_bf[:])
            nc.sync.dma_start(out=word_rows[:, tok], in_=out_words[:, tok].bitcast(I32))
            for u in units:
                nc.scalar.copy(
                    out=out32[:, :, u * UNIT : (u + 1) * UNIT], in_=acc[u][:].rearrange("p (s t) -> p s t", s=PACK)
                )
            queue = nc.scalar if first + width == TOKENS else nc.sync
            queue.dma_start(out=out_rows[:, :, tok], in_=out32[:, :, tok])
        scale_rows = out_2[0].rearrange("(q i) t -> i q t", i=4)
        for i in range(4):
            queue = nc.sync if i < 2 else nc.scalar
            queue.dma_start(out=scale_rows[i].bitcast(I32), in_=out_scales[i:P:32, :].bitcast(I32))
